import numpy as np
import ml_dtypes


def mxq(x, axis, fmt="e4m3"):
    dtype, down = {"e4m3": (ml_dtypes.float8_e4m3fn, 7), "e5m2": (ml_dtypes.float8_e5m2, 14)}[fmt]
    v = np.moveaxis(np.asarray(x, np.float32).astype(ml_dtypes.bfloat16).astype(np.float64), axis, -1)
    blocks = v.reshape(v.shape[:-1] + (-1, 32))
    amax = np.abs(blocks).max(-1, keepdims=True)
    byte = np.maximum(np.where(amax > 0, np.frexp(amax)[1] - 1 + 127, 0) - down, 1)
    scale = np.exp2(byte - 127.0)
    codes = (blocks / scale).astype(np.float32).astype(dtype).astype(np.float64)
    return np.moveaxis((codes * scale).reshape(v.shape), -1, axis)


WIDE = False


def mx_kscale(k):
    if not WIDE:
        return np.ones(k)
    levels = np.array([10, -10, 5, -5, 0])
    if k % 512:
        return np.exp2(np.random.permutation(np.resize(levels, k // 32))).repeat(32)
    a = np.empty((k // 512, 16))
    for p in range(k // 512):
        a[p, :8] = np.random.permutation(np.resize(levels, 8))
        for g in range(8):
            far = levels[np.abs(levels - a[p, g]) >= 10]
            a[p, g + 8] = far[np.random.randint(len(far))]
    return np.exp2(a.ravel()).repeat(32)


def f64(x):
    return np.asarray(x).astype(np.float64)


def striped(idx):
    return np.tile(np.asarray(idx).reshape(-1, 16).T, (8, 1)).astype(np.uint16)


def unstriped(offs):
    return offs[:16].T.reshape(-1).astype(np.int64)


E2M1 = np.array([0.0, 0.5, 1.0, 1.5, 2.0, 3.0, 4.0, 6.0, -0.0, -0.5, -1.0, -1.5, -2.0, -3.0, -4.0, -6.0])


def pack_weight(w, fmt):
    k, n = w.shape
    w = f64(np.asarray(w, np.float32).astype(ml_dtypes.bfloat16)).reshape(k // 32, 32, n)
    amax = np.abs(w).max(1)
    if fmt == "e4m3":
        byte = np.frexp(amax)[1] - 1 + 127 - 7
    else:
        mant, ex = np.frexp(amax / 6.0)
        byte = np.where(mant > 0.5, ex, ex - 1) + 127
    byte = np.clip(np.where(amax > 0, byte, 1), 1, 254)
    scaled = (w * np.exp2(127.0 - byte)[:, None, :]).reshape(k, n).astype(np.float32)
    by_word = np.ascontiguousarray(scaled.reshape(k // 512, 128, 4, n).transpose(0, 1, 3, 2))
    if fmt == "e4m3":
        words = by_word.astype(ml_dtypes.float8_e4m3fn).view(np.uint8)
    else:
        c = by_word.astype(ml_dtypes.float4_e2m1fn).view(np.uint8) & 0xF
        words = (c[..., 0::2] | (c[..., 1::2] << 4)).reshape(k // 512, 128, 2 * n)
    return np.ascontiguousarray(words), np.ascontiguousarray(byte.astype(np.uint8).reshape(k // 512, 16, n))


def unpack_weight(words, scales, fmt):
    g, _, n = scales.shape
    words = np.ascontiguousarray(words).reshape(g, 128, n, -1)
    if fmt == "e4m3":
        vals = words.view(ml_dtypes.float8_e4m3fn).astype(np.float64)
    else:
        nib = np.empty((g, 128, n, 4), np.uint8)
        nib[..., 0::2] = words & 0xF
        nib[..., 1::2] = words >> 4
        vals = E2M1[nib]
    vals = vals * np.repeat(np.exp2(scales.astype(np.float64) - 127.0), 8, axis=1)[..., None]
    return vals.transpose(0, 1, 3, 2).reshape(g * 512, n)


def sigmoid(v):
    return 1.0 / (1.0 + np.exp(-v))


D, K, R, T, I, Q, U = 512, 512, 512, 2048, 512, 128, 1024


def setup_inputs():
    n = np.random.standard_normal
    idx2 = np.random.permutation(U)[:I]
    idx = np.random.permutation(T)[:I]
    fd = mx_kscale(D)
    fk = mx_kscale(K)
    fi = mx_kscale(I)
    keysp = pack_weight(n((D, T)) / fd[:, None], "e2m1")
    tabp = pack_weight(n((K, T)) / fk[:, None], "e2m1")
    return {
        "query": (n((D, Q)) * 0.7 / np.sqrt(D) * fd[:, None]).astype(np.float32),
        "keys_words": keysp[0],
        "keys_scales": keysp[1],
        "tab_words": tabp[0],
        "tab_scales": tabp[1],
        "w1": (n((K, R)) * 1 / np.sqrt(K) * fk[:, None]).astype(np.float32),
        "gtab": (n((R, U))).astype(np.float32),
        "os": (np.random.uniform(4.0, 16.0, (1, I)) * fi).astype(np.float32),
        "vs": (np.random.uniform(0.5, 2.0, (1, I)) / fi).astype(np.float32),
        "offs2": striped(idx2),
        "offs": striped(idx),
    }


def reference(query, keys_words, keys_scales, tab_words, tab_scales, w1, gtab, os, vs, offs2, offs):
    idx2 = unstriped(offs2)
    idx = unstriped(offs)
    keysu = unpack_weight(keys_words, keys_scales, "e2m1")
    tabu = unpack_weight(tab_words, tab_scales, "e2m1")
    queryq = mxq(f64(query), 0, "e4m3")
    keysidxg = keysu[:, idx]
    a = queryq.T @ keysidxg
    p = np.exp(a - np.max(a, axis=1, keepdims=True))
    z = np.sum(p, axis=1, keepdims=True)
    w = p / z
    w1q = mxq(f64(w1), 0, "e4m3")
    tabidxg = tabu[:, idx]
    zh = w1q.T @ tabidxg
    hg = sigmoid(f64(gtab)[:, idx2])
    hv = zh * hg
    wo1 = w * f64(os)
    wt1 = wo1.T
    hw = hv * f64(vs)
    ht1 = hw.T
    wt1q = mxq(wt1, 0, "e4m3")
    ht1q = mxq(ht1, 0, "e4m3")
    o = wt1q.T @ ht1q
    return o

@@ -1,0 +1,236 @@
+from contextlib import ExitStack
+
+import concourse.mybir as mybir
+from concourse.masks import make_identity
+
+D, K, R, T, I, Q, U = 512, 512, 512, 2048, 512, 128, 1024
+FLOPS = 2 * (D * Q * I + K * R * I + I * Q * R)
+
+F32 = mybir.dt.float32
+BF16 = mybir.dt.bfloat16
+I32 = mybir.dt.int32
+U32 = mybir.dt.uint32
+U16 = mybir.dt.uint16
+U8 = mybir.dt.uint8
+FP8X4 = mybir.dt.float8_e4m3fn_x4
+FP4X4 = mybir.dt.float4_e2m1fn_x4
+ACT = mybir.ActivationFunctionType
+MULT = mybir.AluOpType.mult
+ADD = mybir.AluOpType.add
+MAX = mybir.AluOpType.max
+AXIS_X = mybir.AxisListType.X
+
+P = 128
+PACK = 4
+HALF = R // 2
+NBLK = R // P
+
+
+def tile_attend_lrgated_soft_kernel(tc, query, keys_words, keys_scales, tab_words, tab_scales,
+                                     w1, gtab, os_in, vs_in, offs2, offs, out):
+    nc = tc.nc
+    with ExitStack() as ctx:
+        lists = ctx.enter_context(tc.tile_pool(name="lists", bufs=1))
+        sb = ctx.enter_context(tc.tile_pool(name="sb", bufs=1))
+        ps = ctx.enter_context(tc.psum_pool(name="ps", bufs=1))
+
+        def sbuf(name, shape, dtype):
+            return sb.tile(shape, dtype, name=name, align_bytes=64)
+
+        def load_scales(queue, window, scales):
+            for quad in range(4):
+                queue.dma_start(
+                    out=window[32 * quad : 32 * quad + 4, :].bitcast(I32),
+                    in_=scales[0, 4 * quad : 4 * quad + 4, :].bitcast(I32),
+                )
+
+        def interleave(dst, src):
+            nc.gpsimd.tensor_scalar(out=dst, in0=src.rearrange("p t c -> p c t"), scalar1=1.0, scalar2=0.0,
+                                    op0=MULT, op1=ADD)
+
+        tok_list = lists.tile([P, I // 16], U16, name="tok_list")
+        gate_list = lists.tile([P, I // 16], U16, name="gate_list")
+
+        ks_pool = sbuf("ks_pool", [P, T], U8)
+        ts_pool = sbuf("ts_pool", [P, T], U8)
+        kw_pool = sbuf("kw_pool", [P, T], U16)
+        tw_pool = sbuf("tw_pool", [P, T], U16)
+        nc.vector.memset(ks_pool[:].bitcast(I32), 0)
+
+        warm = sbuf("g_pool1", [P, 1], F32)
+        warm_out = sbuf("q_raw", [P, 1], F32)
+        nc.vector.memset(warm[:], 0.0)
+        nc.scalar.activation(warm_out[:], warm[:], ACT.Sigmoid)
+
+        vs_col = sbuf("vs_col", [P, PACK], F32)
+        os_col = sbuf("os_col", [P, PACK], F32)
+        nc.gpsimd.dma_start(out=vs_col[:], in_=vs_in.rearrange("o (p t) -> (o p) t", t=PACK))
+        ident = sbuf("ident", [P, P], F32)
+        make_identity(nc, ident[:])
+        nc.gpsimd.dma_start(out=os_col[:], in_=os_in.rearrange("o (p t) -> (o p) t", t=PACK))
+
+        nc.gpsimd.memset(ts_pool[:].bitcast(I32), 0)
+        g_pool = [None] * NBLK
+        q_raw = sbuf("q_raw", [P, PACK, Q], F32)
+        w_raw = [None] * 2
+        w1_rows = w1.rearrange("(p t) r -> p t r", t=PACK)
+
+        def load_gate(j):
+            g_pool[j] = sbuf(("g_pool0", "g_pool1", "tw_pool", "g_pool0")[j], [P, U], F32)
+            nc.sync.dma_start(out=g_pool[j][:], in_=gtab[j * P : (j + 1) * P, :])
+
+        def load_w1(h):
+            w_raw[h] = sbuf(("kw_pool", "g_pool1")[h], [P, PACK, HALF], F32)
+            nc.sync.dma_start(out=w_raw[h][:], in_=w1_rows[:, :, h * HALF : (h + 1) * HALF])
+
+        nc.sync.dma_start(tok_list[:], offs)
+        nc.sync.dma_start(out=kw_pool[:].bitcast(I32), in_=keys_words[0].bitcast(I32))
+        nc.sync.dma_start(out=tw_pool[:].bitcast(I32), in_=tab_words[0].bitcast(I32))
+        load_gate(0)
+        nc.sync.dma_start(gate_list[:], offs2)
+        load_scales(nc.sync, ks_pool, keys_scales)
+        load_gate(1)
+        nc.sync.dma_start(out=q_raw[:], in_=query.rearrange("(p t) q -> p t q", t=PACK))
+        load_scales(nc.sync, ts_pool, tab_scales)
+
+        kw = sbuf("kw", [P, I], U16)
+        ks = sbuf("ks", [P, I], U8)
+        tw = sbuf("tw", [P, I], U16)
+        ts = sbuf("ts", [P, I], U8)
+        nc.vector.tensor_copy(kw[:], kw_pool[:].indirect(tok_list[:]))
+        load_w1(0)
+        nc.vector.tensor_copy(tw[:], tw_pool[:].indirect(tok_list[:]))
+        load_gate(2)
+        tw_dealt = sbuf("tw_dealt", [P, PACK, P], U16)
+        nc.vector.tensor_copy(out=tw_dealt[:], in_=tw[:].rearrange("p (s t) -> p t s", t=PACK))
+        nc.vector.tensor_copy(ks[:], ks_pool[:].indirect(tok_list[:]))
+        nc.vector.tensor_copy(ts[:], ts_pool[:].indirect(tok_list[:]))
+        ts_dealt = sbuf("ts_dealt", [P, PACK, P], U8)
+        nc.vector.tensor_copy(out=ts_dealt[:], in_=ts[:].rearrange("p (s t) -> p t s", t=PACK))
+
+        gate = [None] * NBLK
+        gate_v = [None] * NBLK
+        gate_ps = [None] * NBLK
+
+        def gather_gate(j):
+            if j % 2 == 0:
+                pair = sbuf("gate_pair", [P, 2, I], F32)
+                gate[j], gate[j + 1] = pair[:, 0, :], pair[:, 1, :]
+            nc.scalar.activation(gate[j], g_pool[j][:].indirect(gate_list[:]), ACT.Sigmoid)
+
+        def turn_gate(j):
+            gate_ps[j] = ps.tile([P, PACK, P], F32, name="gate_ps", tag="bank%d" % (0, 1, 6, 7)[j])
+            for t in range(PACK):
+                nc.tensor.transpose(gate_ps[j][:, t, :], gate[j][:, t::PACK], ident[:])
+
+        def scale_gates_scalar(j):
+            tile = sbuf(("gate_v0", "gate_v1", None, "neg_max")[j], [P, PACK, P], F32)
+            for t in range(PACK):
+                nc.scalar.activation(tile[:, t, :], gate_ps[j][:, t, :], ACT.Copy, scale=vs_col[:, t : t + 1])
+            gate_v[j] = tile[:].rearrange("p t r -> p r t")
+
+        def scale_gates_vector(j):
+            tile = sbuf("gate_v%d" % j, [P, P, PACK], F32)
+            nc.vector.tensor_tensor(out=tile[:], in0=gate_ps[j][:].rearrange("p t r -> p r t"),
+                                    in1=vs_col[:].unsqueeze(1).to_broadcast([P, P, PACK]), op=MULT)
+            gate_v[j] = tile[:]
+
+        gather_gate(0)
+        load_gate(3)
+        turn_gate(0)
+        gather_gate(1)
+        load_w1(1)
+        turn_gate(1)
+
+        q_bf = sbuf("q_bf", [P, Q, PACK], BF16)
+        interleave(q_bf[:], q_raw[:])
+        q_codes = sbuf("q_codes", [P, Q], U32)
+        q_scales = sbuf("q_scales", [P, Q], U8)
+        nc.vector.quantize_mx(out=q_codes[:].bitcast(FP8X4), scales=q_scales[:],
+                              in_=q_bf[:].rearrange("p q t -> p (q t)"))
+        scores = ps.tile([P, I], F32, name="scores", tag="bank4")
+        nc.tensor.matmul_mx(out=scores[:], lhsT=q_codes[:].bitcast(FP8X4), lhsT_scale=q_scales[:],
+                            rhs=kw[:].bitcast(FP4X4), rhs_scale=ks[:], start=True, stop=True)
+        neg_max = sbuf("neg_max", [P, 1], F32)
+        nc.vector.tensor_reduce(out=neg_max[:], in_=scores[:], axis=AXIS_X, op=MAX, negate=True)
+
+        os_rows = ps.tile([P, PACK, P], F32, name="os_rows", tag="bank5")
+        for t in range(PACK):
+            nc.tensor.transpose(os_rows[:, t, :], os_col[:, t : t + 1].to_broadcast([P, P]), ident[:])
+
+        scale_gates_scalar(0)
+        scale_gates_scalar(1)
+        gather_gate(2)
+        gather_gate(3)
+
+        probs = sb.tile([P, 2, P, 2], F32, name="probs", tag="g_pool0", align_bytes=64)
+        row_sum = sbuf("row_sum", [P, 1], F32)
+        nc.scalar.activation(probs[:], scores[:].rearrange("q (s u e) -> q u s e", u=2, e=2), ACT.Exp,
+                             bias=neg_max[:], accum_out=row_sum[:])
+
+        w_codes = [None] * 2
+        w_scales = [sbuf("w_scales%d" % h, [P, HALF], U8) for h in range(2)]
+        h_bf = [sbuf("h_bf%d" % h, [P, HALF, PACK], BF16) for h in range(2)]
+        h_codes = [sbuf("h_codes%d" % h, [P, HALF], U32) for h in range(2)]
+        h_scales = [sbuf("h_scales%d" % h, [P, HALF], U8) for h in range(2)]
+
+        def quantise_w1(h):
+            w_bf = sbuf("w_bf%d" % h, [P, HALF, PACK], BF16)
+            interleave(w_bf[:], w_raw[h][:])
+            w_codes[h] = sbuf(("w_codes0", "gate_v1")[h], [P, HALF], U32)
+            nc.vector.quantize_mx(out=w_codes[h][:].bitcast(FP8X4), scales=w_scales[h][:],
+                                  in_=w_bf[:].rearrange("p r t -> p (r t)"))
+
+        def layer_block(j):
+            h, jj = divmod(j, 2)
+            cols = slice(jj * P, (jj + 1) * P)
+            zh = ps.tile([P, PACK, P], F32, name="zh", tag="bank%d" % (6, 7, 0, 1)[j])
+            for t in range(PACK):
+                nc.tensor.matmul_mx(out=zh[:, t, :], lhsT=tw_dealt[:, t, :].bitcast(FP4X4),
+                                    lhsT_scale=ts_dealt[:, t, :], rhs=w_codes[h][:, cols].bitcast(FP8X4),
+                                    rhs_scale=w_scales[h][:, cols], start=True, stop=True)
+            nc.vector.tensor_tensor(out=h_bf[h][:, cols, :], in0=zh[:].rearrange("p t r -> p r t"),
+                                    in1=gate_v[j], op=MULT)
+
+        def quantise_half(h):
+            nc.vector.quantize_mx(out=h_codes[h][:].bitcast(FP8X4), scales=h_scales[h][:],
+                                  in_=h_bf[h][:].rearrange("p r t -> p (r t)"))
+
+        quantise_w1(0)
+        layer_block(0)
+        layer_block(1)
+        turn_gate(2)
+        turn_gate(3)
+        scale_gates_scalar(3)
+        quantise_w1(1)
+        quantise_half(0)
+        scale_gates_vector(2)
+        layer_block(2)
+
+        inv_sum = sbuf("inv_sum", [P, 1], F32)
+        nc.vector.reciprocal(out=inv_sum[:], in_=row_sum[:])
+        wo_bf = sbuf("wo_bf", [P, 2, P, 2], BF16)
+        wo_ps = ps.tile([P, 2, P], F32, name="wo_ps", tag="bank4")
+        wo_words = wo_bf[:].rearrange("q u s e -> q u (s e)").bitcast(F32)
+        for u in range(2):
+            nc.vector.scalar_tensor_tensor(
+                out=wo_bf[:, u], in0=probs[:, u], scalar=inv_sum[:],
+                in1=os_rows[:, 2 * u : 2 * u + 2, :].rearrange("q e s -> q s e"), op0=MULT, op1=MULT)
+            nc.tensor.transpose(wo_ps[:, u, :], wo_words[:, u, :], ident[:])
+        wt_bf = sbuf("wt_bf", [P, Q, PACK], BF16)
+        nc.scalar.copy(out=wt_bf[:].bitcast(F32), in_=wo_ps[:].rearrange("s u q -> s q u"))
+        layer_block(3)
+        wt_codes = sbuf("wt_codes", [P, Q], U32)
+        wt_scales = sbuf("wt_scales", [P, Q], U8)
+        nc.vector.quantize_mx(out=wt_codes[:].bitcast(FP8X4), scales=wt_scales[:],
+                              in_=wt_bf[:].rearrange("p q t -> p (q t)"))
+        quantise_half(1)
+
+        for h, copy_out in enumerate((nc.scalar.copy, nc.vector.tensor_copy)):
+            acc = ps.tile([P, HALF], F32, name="acc", tag="bank%d" % (2 + h))
+            nc.tensor.matmul_mx(out=acc[:], lhsT=wt_codes[:].bitcast(FP8X4), lhsT_scale=wt_scales[:],
+                                rhs=h_codes[h][:].bitcast(FP8X4), rhs_scale=h_scales[h][:],
+                                start=True, stop=True)
+            result = sbuf("result%d" % h, [P, HALF], F32)
+            copy_out(out=result[:], in_=acc[:])
+            nc.sync.dma_start(out=out[:, h * HALF : (h + 1) * HALF], in_=result[:])

@@ -16,7 +16,6 @@ FP8X4 = mybir.dt.float8_e4m3fn_x4
 FP4X4 = mybir.dt.float4_e2m1fn_x4
 ACT = mybir.ActivationFunctionType
 MULT = mybir.AluOpType.mult
-ADD = mybir.AluOpType.add
 MAX = mybir.AluOpType.max
 AXIS_X = mybir.AxisListType.X
 
@@ -34,8 +33,11 @@ def tile_attend_lrgated_soft_kernel(tc, query, keys_words, keys_scales, tab_word
         sb = ctx.enter_context(tc.tile_pool(name="sb", bufs=1))
         ps = ctx.enter_context(tc.psum_pool(name="ps", bufs=1))
 
-        def sbuf(name, shape, dtype):
-            return sb.tile(shape, dtype, name=name, align_bytes=64)
+        def sbuf(name, shape, dtype, buffer=None):
+            return sb.tile(shape, dtype, name=name, tag=buffer or name, align_bytes=64)
+
+        def bank(name, shape, number):
+            return ps.tile(shape, F32, name=name, tag="bank%d" % number)
 
         def load_scales(queue, window, scales):
             for quad in range(4):
@@ -44,193 +46,169 @@ def tile_attend_lrgated_soft_kernel(tc, query, keys_words, keys_scales, tab_word
                     in_=scales[0, 4 * quad : 4 * quad + 4, :].bitcast(I32),
                 )
 
-        def interleave(dst, src):
-            nc.gpsimd.tensor_scalar(out=dst, in0=src.rearrange("p t c -> p c t"), scalar1=1.0, scalar2=0.0,
-                                    op0=MULT, op1=ADD)
+        def interleave(engine_copy, dst, src):
+            engine_copy(
+                out=dst.rearrange("p (c i) t -> p c t i", i=4),
+                in_=src.rearrange("p t (c i) -> p c t i", i=4),
+            )
+
+        def quantise(codes, scales, values):
+            nc.vector.quantize_mx(out=codes.bitcast(FP8X4), scales=scales,
+                                  in_=values.rearrange("p c t -> p (c t)"))
 
         tok_list = lists.tile([P, I // 16], U16, name="tok_list")
         gate_list = lists.tile([P, I // 16], U16, name="gate_list")
 
+        warm_in = sbuf("warm_in", [P, 1], F32, "tw_pool")
+        warm_out = sbuf("warm_out", [P, 1], F32, "w_raw")
+        nc.vector.memset(warm_in[:], 0.0)
+        nc.scalar.activation(warm_out[:], warm_in[:], ACT.Exp)
+
         ks_pool = sbuf("ks_pool", [P, T], U8)
         ts_pool = sbuf("ts_pool", [P, T], U8)
-        kw_pool = sbuf("kw_pool", [P, T], U16)
-        tw_pool = sbuf("tw_pool", [P, T], U16)
         nc.vector.memset(ks_pool[:].bitcast(I32), 0)
-
-        warm = sbuf("g_pool1", [P, 1], F32)
-        warm_out = sbuf("q_raw", [P, 1], F32)
-        nc.vector.memset(warm[:], 0.0)
-        nc.scalar.activation(warm_out[:], warm[:], ACT.Sigmoid)
-
+        nc.gpsimd.memset(ts_pool[:].bitcast(I32), 0)
+        load_scales(nc.gpsimd, ts_pool, tab_scales)
         vs_col = sbuf("vs_col", [P, PACK], F32)
         os_col = sbuf("os_col", [P, PACK], F32)
         nc.gpsimd.dma_start(out=vs_col[:], in_=vs_in.rearrange("o (p t) -> (o p) t", t=PACK))
+        nc.gpsimd.dma_start(out=os_col[:], in_=os_in.rearrange("o (p t) -> (o p) t", t=PACK))
         ident = sbuf("ident", [P, P], F32)
         make_identity(nc, ident[:])
-        nc.gpsimd.dma_start(out=os_col[:], in_=os_in.rearrange("o (p t) -> (o p) t", t=PACK))
 
-        nc.gpsimd.memset(ts_pool[:].bitcast(I32), 0)
-        g_pool = [None] * NBLK
+        kw_pool = sbuf("kw_pool", [P, T], U16)
+        tw_pool = sbuf("tw_pool", [P, T], U16)
         q_raw = sbuf("q_raw", [P, PACK, Q], F32)
-        w_raw = [None] * 2
+        w_raw = sbuf("w_raw", [P, 2, PACK, HALF], F32)
         w1_rows = w1.rearrange("(p t) r -> p t r", t=PACK)
-
-        def load_gate(j):
-            g_pool[j] = sbuf(("g_pool0", "g_pool1", "tw_pool", "g_pool0")[j], [P, U], F32)
-            nc.sync.dma_start(out=g_pool[j][:], in_=gtab[j * P : (j + 1) * P, :])
-
-        def load_w1(h):
-            w_raw[h] = sbuf(("kw_pool", "g_pool1")[h], [P, PACK, HALF], F32)
-            nc.sync.dma_start(out=w_raw[h][:], in_=w1_rows[:, :, h * HALF : (h + 1) * HALF])
-
         nc.sync.dma_start(tok_list[:], offs)
         nc.sync.dma_start(out=kw_pool[:].bitcast(I32), in_=keys_words[0].bitcast(I32))
-        nc.sync.dma_start(out=tw_pool[:].bitcast(I32), in_=tab_words[0].bitcast(I32))
-        load_gate(0)
         nc.sync.dma_start(gate_list[:], offs2)
-        load_scales(nc.sync, ks_pool, keys_scales)
-        load_gate(1)
         nc.sync.dma_start(out=q_raw[:], in_=query.rearrange("(p t) q -> p t q", t=PACK))
-        load_scales(nc.sync, ts_pool, tab_scales)
+        load_scales(nc.sync, ks_pool, keys_scales)
+        nc.sync.dma_start(out=tw_pool[:].bitcast(I32), in_=tab_words[0].bitcast(I32))
+        for h in range(2):
+            nc.sync.dma_start(out=w_raw[:, h], in_=w1_rows[:, :, h * HALF : (h + 1) * HALF])
+
+        g_pool = []
+
+        def load_gates(freed_buffer):
+            j = len(g_pool)
+            g_pool.append(sbuf("g_pool", [P, U], F32, freed_buffer))
+            nc.sync.dma_start(out=g_pool[j][:], in_=gtab[j * P : (j + 1) * P, :])
 
         kw = sbuf("kw", [P, I], U16)
         ks = sbuf("ks", [P, I], U8)
-        tw = sbuf("tw", [P, I], U16)
-        ts = sbuf("ts", [P, I], U8)
         nc.vector.tensor_copy(kw[:], kw_pool[:].indirect(tok_list[:]))
-        load_w1(0)
-        nc.vector.tensor_copy(tw[:], tw_pool[:].indirect(tok_list[:]))
-        load_gate(2)
-        tw_dealt = sbuf("tw_dealt", [P, PACK, P], U16)
-        nc.vector.tensor_copy(out=tw_dealt[:], in_=tw[:].rearrange("p (s t) -> p t s", t=PACK))
-        nc.vector.tensor_copy(ks[:], ks_pool[:].indirect(tok_list[:]))
-        nc.vector.tensor_copy(ts[:], ts_pool[:].indirect(tok_list[:]))
-        ts_dealt = sbuf("ts_dealt", [P, PACK, P], U8)
-        nc.vector.tensor_copy(out=ts_dealt[:], in_=ts[:].rearrange("p (s t) -> p t s", t=PACK))
-
-        gate = [None] * NBLK
-        gate_v = [None] * NBLK
-        gate_ps = [None] * NBLK
-
-        def gather_gate(j):
-            if j % 2 == 0:
-                pair = sbuf("gate_pair", [P, 2, I], F32)
-                gate[j], gate[j + 1] = pair[:, 0, :], pair[:, 1, :]
-            nc.scalar.activation(gate[j], g_pool[j][:].indirect(gate_list[:]), ACT.Sigmoid)
-
-        def turn_gate(j):
-            gate_ps[j] = ps.tile([P, PACK, P], F32, name="gate_ps", tag="bank%d" % (0, 1, 6, 7)[j])
-            for t in range(PACK):
-                nc.tensor.transpose(gate_ps[j][:, t, :], gate[j][:, t::PACK], ident[:])
-
-        def scale_gates_scalar(j):
-            tile = sbuf(("gate_v0", "gate_v1", None, "neg_max")[j], [P, PACK, P], F32)
-            for t in range(PACK):
-                nc.scalar.activation(tile[:, t, :], gate_ps[j][:, t, :], ACT.Copy, scale=vs_col[:, t : t + 1])
-            gate_v[j] = tile[:].rearrange("p t r -> p r t")
-
-        def scale_gates_vector(j):
-            tile = sbuf("gate_v%d" % j, [P, P, PACK], F32)
-            nc.vector.tensor_tensor(out=tile[:], in0=gate_ps[j][:].rearrange("p t r -> p r t"),
-                                    in1=vs_col[:].unsqueeze(1).to_broadcast([P, P, PACK]), op=MULT)
-            gate_v[j] = tile[:]
-
-        gather_gate(0)
-        load_gate(3)
-        turn_gate(0)
-        gather_gate(1)
-        load_w1(1)
-        turn_gate(1)
-
+        load_gates("kw_pool")
         q_bf = sbuf("q_bf", [P, Q, PACK], BF16)
-        interleave(q_bf[:], q_raw[:])
+        interleave(nc.scalar.copy, q_bf[:], q_raw[:])
+        load_gates("q_raw")
+        nc.vector.tensor_copy(ks[:], ks_pool[:].indirect(tok_list[:]))
+        load_gates("ks_pool")
+
         q_codes = sbuf("q_codes", [P, Q], U32)
         q_scales = sbuf("q_scales", [P, Q], U8)
-        nc.vector.quantize_mx(out=q_codes[:].bitcast(FP8X4), scales=q_scales[:],
-                              in_=q_bf[:].rearrange("p q t -> p (q t)"))
-        scores = ps.tile([P, I], F32, name="scores", tag="bank4")
+        quantise(q_codes[:], q_scales[:], q_bf[:])
+        scores = bank("scores", [P, I], 0)
         nc.tensor.matmul_mx(out=scores[:], lhsT=q_codes[:].bitcast(FP8X4), lhsT_scale=q_scales[:],
                             rhs=kw[:].bitcast(FP4X4), rhs_scale=ks[:], start=True, stop=True)
+
+        tw = sbuf("tw", [P, I], U16)
+        nc.vector.tensor_copy(tw[:], tw_pool[:].indirect(tok_list[:]))
+        load_gates("tw_pool")
+
+        w_bf = [sbuf("w_bf%d" % h, [P, HALF, PACK], BF16) for h in range(2)]
+        interleave(nc.scalar.copy, w_bf[0][:], w_raw[:, 0])
+
         neg_max = sbuf("neg_max", [P, 1], F32)
         nc.vector.tensor_reduce(out=neg_max[:], in_=scores[:], axis=AXIS_X, op=MAX, negate=True)
-
-        os_rows = ps.tile([P, PACK, P], F32, name="os_rows", tag="bank5")
-        for t in range(PACK):
-            nc.tensor.transpose(os_rows[:, t, :], os_col[:, t : t + 1].to_broadcast([P, P]), ident[:])
-
-        scale_gates_scalar(0)
-        scale_gates_scalar(1)
-        gather_gate(2)
-        gather_gate(3)
-
-        probs = sb.tile([P, 2, P, 2], F32, name="probs", tag="g_pool0", align_bytes=64)
+        probs = sbuf("probs", [P, 2, P, 2], F32)
         row_sum = sbuf("row_sum", [P, 1], F32)
         nc.scalar.activation(probs[:], scores[:].rearrange("q (s u e) -> q u s e", u=2, e=2), ACT.Exp,
                              bias=neg_max[:], accum_out=row_sum[:])
 
-        w_codes = [None] * 2
-        w_scales = [sbuf("w_scales%d" % h, [P, HALF], U8) for h in range(2)]
-        h_bf = [sbuf("h_bf%d" % h, [P, HALF, PACK], BF16) for h in range(2)]
-        h_codes = [sbuf("h_codes%d" % h, [P, HALF], U32) for h in range(2)]
-        h_scales = [sbuf("h_scales%d" % h, [P, HALF], U8) for h in range(2)]
+        gates = sbuf("gates", [P, NBLK, I], F32, "neg_max")
+        for j in range(NBLK):
+            nc.scalar.activation(gates[:, j, :], g_pool[j][:].indirect(gate_list[:]), ACT.Sigmoid)
 
-        def quantise_w1(h):
-            w_bf = sbuf("w_bf%d" % h, [P, HALF, PACK], BF16)
-            interleave(w_bf[:], w_raw[h][:])
-            w_codes[h] = sbuf(("w_codes0", "gate_v1")[h], [P, HALF], U32)
-            nc.vector.quantize_mx(out=w_codes[h][:].bitcast(FP8X4), scales=w_scales[h][:],
-                                  in_=w_bf[:].rearrange("p r t -> p (r t)"))
-
-        def layer_block(j):
-            h, jj = divmod(j, 2)
-            cols = slice(jj * P, (jj + 1) * P)
-            zh = ps.tile([P, PACK, P], F32, name="zh", tag="bank%d" % (6, 7, 0, 1)[j])
-            for t in range(PACK):
-                nc.tensor.matmul_mx(out=zh[:, t, :], lhsT=tw_dealt[:, t, :].bitcast(FP4X4),
-                                    lhsT_scale=ts_dealt[:, t, :], rhs=w_codes[h][:, cols].bitcast(FP8X4),
-                                    rhs_scale=w_scales[h][:, cols], start=True, stop=True)
-            nc.vector.tensor_tensor(out=h_bf[h][:, cols, :], in0=zh[:].rearrange("p t r -> p r t"),
-                                    in1=gate_v[j], op=MULT)
-
-        def quantise_half(h):
-            nc.vector.quantize_mx(out=h_codes[h][:].bitcast(FP8X4), scales=h_scales[h][:],
-                                  in_=h_bf[h][:].rearrange("p r t -> p (r t)"))
-
-        quantise_w1(0)
-        layer_block(0)
-        layer_block(1)
-        turn_gate(2)
-        turn_gate(3)
-        scale_gates_scalar(3)
-        quantise_w1(1)
-        quantise_half(0)
-        scale_gates_vector(2)
-        layer_block(2)
-
+        tw_dealt = sbuf("tw_dealt", [P, PACK, P], U16)
+        nc.vector.tensor_copy(out=tw_dealt[:], in_=tw[:].rearrange("p (s t) -> p t s", t=PACK))
+        ts = sbuf("ts", [P, I], U8, "tw")
+        nc.vector.tensor_copy(ts[:], ts_pool[:].indirect(tok_list[:]))
+        w_codes = sbuf("w_codes", [P, R], U32)
+        w_scales = sbuf("w_scales", [P, R], U8)
+        quantise(w_codes[:, :HALF], w_scales[:, :HALF], w_bf[0][:])
+        ts_dealt = sbuf("ts_dealt", [P, PACK, P], U8)
+        nc.vector.tensor_copy(out=ts_dealt[:], in_=ts[:].rearrange("p (s t) -> p t s", t=PACK))
+        interleave(nc.vector.tensor_copy, w_bf[1][:], w_raw[:, 1])
         inv_sum = sbuf("inv_sum", [P, 1], F32)
         nc.vector.reciprocal(out=inv_sum[:], in_=row_sum[:])
+        quantise(w_codes[:, HALF:], w_scales[:, HALF:], w_bf[1][:])
+
+        zv = []
+        for j in range(NBLK):
+            cols = slice(j * P, (j + 1) * P)
+            zh = bank("zh", [P, PACK, P], 2 + j)
+            for t in range(PACK):
+                nc.tensor.matmul_mx(out=zh[:, t, :], lhsT=tw_dealt[:, t, :].bitcast(FP4X4),
+                                    lhsT_scale=ts_dealt[:, t, :], rhs=w_codes[:, cols].bitcast(FP8X4),
+                                    rhs_scale=w_scales[:, cols], start=True, stop=True)
+            zv.append(sbuf("zv%d" % j, [P, P, PACK], F32))
+            nc.vector.tensor_tensor(out=zv[j][:], in0=zh[:].rearrange("p t r -> p r t"),
+                                    in1=vs_col[:].unsqueeze(1).to_broadcast([P, P, PACK]), op=MULT)
+
+        os_rows = bank("os_rows", [P, PACK, P], 2)
+        for t in range(PACK):
+            nc.tensor.transpose(os_rows[:, t, :], os_col[:, t : t + 1].to_broadcast([P, P]), ident[:])
         wo_bf = sbuf("wo_bf", [P, 2, P, 2], BF16)
-        wo_ps = ps.tile([P, 2, P], F32, name="wo_ps", tag="bank4")
         wo_words = wo_bf[:].rearrange("q u s e -> q u (s e)").bitcast(F32)
+        wo_turned = bank("wo_turned", [P, 2, Q], 1)
         for u in range(2):
             nc.vector.scalar_tensor_tensor(
                 out=wo_bf[:, u], in0=probs[:, u], scalar=inv_sum[:],
                 in1=os_rows[:, 2 * u : 2 * u + 2, :].rearrange("q e s -> q s e"), op0=MULT, op1=MULT)
-            nc.tensor.transpose(wo_ps[:, u, :], wo_words[:, u, :], ident[:])
-        wt_bf = sbuf("wt_bf", [P, Q, PACK], BF16)
-        nc.scalar.copy(out=wt_bf[:].bitcast(F32), in_=wo_ps[:].rearrange("s u q -> s q u"))
-        layer_block(3)
+            nc.tensor.transpose(wo_turned[:, u, :], wo_words[:, u, :], ident[:])
+
+        h_bf = sbuf("h_bf", [P, R, PACK], BF16)
+        h_codes = sbuf("h_codes", [P, R], U32)
+        h_scales = sbuf("h_scales", [P, R], U8)
+
+        def gate_block(j):
+            turned = bank("turned", [P, PACK, P], 2 + (j + 1) % NBLK)
+            for t in range(PACK):
+                nc.tensor.transpose(turned[:, t, :], gates[:, j, t::PACK], ident[:])
+            nc.vector.tensor_tensor(out=h_bf[:, j * P : (j + 1) * P, :], in0=turned[:].rearrange("p t r -> p r t"),
+                                    in1=zv[j][:], op=MULT)
+
+        def quantise_h(cols):
+            quantise(h_codes[:, cols], h_scales[:, cols], h_bf[:, cols, :])
+
+        wt_bf = sbuf("wt_bf", [P, Q, PACK], BF16, "tw_pool")
         wt_codes = sbuf("wt_codes", [P, Q], U32)
         wt_scales = sbuf("wt_scales", [P, Q], U8)
-        nc.vector.quantize_mx(out=wt_codes[:].bitcast(FP8X4), scales=wt_scales[:],
-                              in_=wt_bf[:].rearrange("p q t -> p (q t)"))
-        quantise_half(1)
+        result = [sbuf("result%d" % h, [P, HALF], F32) for h in range(2)]
 
-        for h, copy_out in enumerate((nc.scalar.copy, nc.vector.tensor_copy)):
-            acc = ps.tile([P, HALF], F32, name="acc", tag="bank%d" % (2 + h))
+        def read_out(cols, bank_number, copy_out):
+            width = cols.stop - cols.start
+            acc = bank("acc", [P, width], bank_number)
             nc.tensor.matmul_mx(out=acc[:], lhsT=wt_codes[:].bitcast(FP8X4), lhsT_scale=wt_scales[:],
-                                rhs=h_codes[h][:].bitcast(FP8X4), rhs_scale=h_scales[h][:],
+                                rhs=h_codes[:, cols].bitcast(FP8X4), rhs_scale=h_scales[:, cols],
                                 start=True, stop=True)
-            result = sbuf("result%d" % h, [P, HALF], F32)
-            copy_out(out=result[:], in_=acc[:])
-            nc.sync.dma_start(out=out[:, h * HALF : (h + 1) * HALF], in_=result[:])
+            h, first = divmod(cols.start, HALF)
+            copy_out(out=result[h][:, first : first + width], in_=acc[:])
+
+        gate_block(0)
+        gate_block(1)
+        nc.scalar.copy(out=wt_bf[:].bitcast(F32), in_=wo_turned[:].rearrange("s u q -> s q u"))
+        gate_block(2)
+        quantise_h(slice(0, HALF))
+        quantise(wt_codes[:], wt_scales[:], wt_bf[:])
+        read_out(slice(0, HALF), 6, nc.scalar.copy)
+        nc.sync.dma_start(out=out[:, :HALF], in_=result[0][:])
+        quantise_h(slice(2 * P, 3 * P))
+        read_out(slice(2 * P, 3 * P), 7, nc.scalar.copy)
+        gate_block(3)
+        quantise_h(slice(3 * P, R))
+        read_out(slice(3 * P, R), 1, nc.vector.tensor_copy)
+        nc.sync.dma_start(out=out[:, HALF:], in_=result[1][:])

@@ -39,9 +39,9 @@ def tile_attend_lrgated_soft_kernel(tc, query, keys_words, keys_scales, tab_word
         def bank(name, shape, number):
             return ps.tile(shape, F32, name=name, tag="bank%d" % number)
 
-        def load_scales(queue, window, scales):
+        def load_scales(window, scales):
             for quad in range(4):
-                queue.dma_start(
+                nc.sync.dma_start(
                     out=window[32 * quad : 32 * quad + 4, :].bitcast(I32),
                     in_=scales[0, 4 * quad : 4 * quad + 4, :].bitcast(I32),
                 )
@@ -60,15 +60,17 @@ def tile_attend_lrgated_soft_kernel(tc, query, keys_words, keys_scales, tab_word
         gate_list = lists.tile([P, I // 16], U16, name="gate_list")
 
         warm_in = sbuf("warm_in", [P, 1], F32, "tw_pool")
-        warm_out = sbuf("warm_out", [P, 1], F32, "w_raw")
+        warm_out = sbuf("warm_out", [P, 1], F32, "w_raw0")
+        warm_sum = sbuf("warm_sum", [P, 1], F32, "w_raw1")
+        warm_bias = sbuf("warm_bias", [P, 1], F32, "ts_pool")
         nc.vector.memset(warm_in[:], 0.0)
-        nc.scalar.activation(warm_out[:], warm_in[:], ACT.Exp)
+        nc.vector.memset(warm_bias[:], 0.0)
+        nc.scalar.activation(warm_out[:], warm_in[:], ACT.Exp, bias=warm_bias[:], accum_out=warm_sum[:])
 
         ks_pool = sbuf("ks_pool", [P, T], U8)
         ts_pool = sbuf("ts_pool", [P, T], U8)
         nc.vector.memset(ks_pool[:].bitcast(I32), 0)
-        nc.gpsimd.memset(ts_pool[:].bitcast(I32), 0)
-        load_scales(nc.gpsimd, ts_pool, tab_scales)
+        nc.vector.memset(ts_pool[:].bitcast(I32), 0)
         vs_col = sbuf("vs_col", [P, PACK], F32)
         os_col = sbuf("os_col", [P, PACK], F32)
         nc.gpsimd.dma_start(out=vs_col[:], in_=vs_in.rearrange("o (p t) -> (o p) t", t=PACK))
@@ -79,16 +81,17 @@ def tile_attend_lrgated_soft_kernel(tc, query, keys_words, keys_scales, tab_word
         kw_pool = sbuf("kw_pool", [P, T], U16)
         tw_pool = sbuf("tw_pool", [P, T], U16)
         q_raw = sbuf("q_raw", [P, PACK, Q], F32)
-        w_raw = sbuf("w_raw", [P, 2, PACK, HALF], F32)
+        w_raw = [sbuf("w_raw%d" % h, [P, PACK, HALF], F32) for h in range(2)]
         w1_rows = w1.rearrange("(p t) r -> p t r", t=PACK)
         nc.sync.dma_start(tok_list[:], offs)
         nc.sync.dma_start(out=kw_pool[:].bitcast(I32), in_=keys_words[0].bitcast(I32))
         nc.sync.dma_start(gate_list[:], offs2)
         nc.sync.dma_start(out=q_raw[:], in_=query.rearrange("(p t) q -> p t q", t=PACK))
-        load_scales(nc.sync, ks_pool, keys_scales)
+        load_scales(ks_pool, keys_scales)
         nc.sync.dma_start(out=tw_pool[:].bitcast(I32), in_=tab_words[0].bitcast(I32))
         for h in range(2):
-            nc.sync.dma_start(out=w_raw[:, h], in_=w1_rows[:, :, h * HALF : (h + 1) * HALF])
+            nc.sync.dma_start(out=w_raw[h][:], in_=w1_rows[:, :, h * HALF : (h + 1) * HALF])
+        load_scales(ts_pool, tab_scales)
 
         g_pool = []
 
@@ -119,11 +122,11 @@ def tile_attend_lrgated_soft_kernel(tc, query, keys_words, keys_scales, tab_word
         load_gates("tw_pool")
 
         w_bf = [sbuf("w_bf%d" % h, [P, HALF, PACK], BF16) for h in range(2)]
-        interleave(nc.scalar.copy, w_bf[0][:], w_raw[:, 0])
+        interleave(nc.scalar.copy, w_bf[0][:], w_raw[0][:])
 
         neg_max = sbuf("neg_max", [P, 1], F32)
         nc.vector.tensor_reduce(out=neg_max[:], in_=scores[:], axis=AXIS_X, op=MAX, negate=True)
-        probs = sbuf("probs", [P, 2, P, 2], F32)
+        probs = sbuf("probs", [P, 2, P, 2], F32, "w_raw0")
         row_sum = sbuf("row_sum", [P, 1], F32)
         nc.scalar.activation(probs[:], scores[:].rearrange("q (s u e) -> q u s e", u=2, e=2), ACT.Exp,
                              bias=neg_max[:], accum_out=row_sum[:])
@@ -136,24 +139,24 @@ def tile_attend_lrgated_soft_kernel(tc, query, keys_words, keys_scales, tab_word
         nc.vector.tensor_copy(out=tw_dealt[:], in_=tw[:].rearrange("p (s t) -> p t s", t=PACK))
         ts = sbuf("ts", [P, I], U8, "tw")
         nc.vector.tensor_copy(ts[:], ts_pool[:].indirect(tok_list[:]))
-        w_codes = sbuf("w_codes", [P, R], U32)
-        w_scales = sbuf("w_scales", [P, R], U8)
-        quantise(w_codes[:, :HALF], w_scales[:, :HALF], w_bf[0][:])
+        w_codes = [sbuf("w_codes%d" % h, [P, HALF], U32) for h in range(2)]
+        w_scales = [sbuf("w_scales%d" % h, [P, HALF], U8) for h in range(2)]
+        quantise(w_codes[0][:], w_scales[0][:], w_bf[0][:])
         ts_dealt = sbuf("ts_dealt", [P, PACK, P], U8)
         nc.vector.tensor_copy(out=ts_dealt[:], in_=ts[:].rearrange("p (s t) -> p t s", t=PACK))
-        interleave(nc.vector.tensor_copy, w_bf[1][:], w_raw[:, 1])
+        interleave(nc.vector.tensor_copy, w_bf[1][:], w_raw[1][:])
         inv_sum = sbuf("inv_sum", [P, 1], F32)
         nc.vector.reciprocal(out=inv_sum[:], in_=row_sum[:])
-        quantise(w_codes[:, HALF:], w_scales[:, HALF:], w_bf[1][:])
+        quantise(w_codes[1][:], w_scales[1][:], w_bf[1][:])
 
         zv = []
         for j in range(NBLK):
-            cols = slice(j * P, (j + 1) * P)
+            h, cols = j // 2, slice(j % 2 * P, (j % 2 + 1) * P)
             zh = bank("zh", [P, PACK, P], 2 + j)
             for t in range(PACK):
                 nc.tensor.matmul_mx(out=zh[:, t, :], lhsT=tw_dealt[:, t, :].bitcast(FP4X4),
-                                    lhsT_scale=ts_dealt[:, t, :], rhs=w_codes[:, cols].bitcast(FP8X4),
-                                    rhs_scale=w_scales[:, cols], start=True, stop=True)
+                                    lhsT_scale=ts_dealt[:, t, :], rhs=w_codes[h][:, cols].bitcast(FP8X4),
+                                    rhs_scale=w_scales[h][:, cols], start=True, stop=True)
             zv.append(sbuf("zv%d" % j, [P, P, PACK], F32))
             nc.vector.tensor_tensor(out=zv[j][:], in0=zh[:].rearrange("p t r -> p r t"),
                                     in1=vs_col[:].unsqueeze(1).to_broadcast([P, P, PACK]), op=MULT)

from contextlib import ExitStack

import concourse.mybir as mybir
from concourse.masks import make_identity

D, K, R, T, I, Q, U = 512, 512, 512, 2048, 512, 128, 1024
FLOPS = 2 * (D * Q * I + K * R * I + I * Q * R)

F32 = mybir.dt.float32
BF16 = mybir.dt.bfloat16
I32 = mybir.dt.int32
U32 = mybir.dt.uint32
U16 = mybir.dt.uint16
U8 = mybir.dt.uint8
FP8X4 = mybir.dt.float8_e4m3fn_x4
FP4X4 = mybir.dt.float4_e2m1fn_x4
ACT = mybir.ActivationFunctionType
MULT = mybir.AluOpType.mult
MAX = mybir.AluOpType.max
AXIS_X = mybir.AxisListType.X

P = 128
PACK = 4
HALF = R // 2
NBLK = R // P


def tile_attend_lrgated_soft_kernel(tc, query, keys_words, keys_scales, tab_words, tab_scales,
                                     w1, gtab, os_in, vs_in, offs2, offs, out):
    nc = tc.nc
    with ExitStack() as ctx:
        lists = ctx.enter_context(tc.tile_pool(name="lists", bufs=1))
        sb = ctx.enter_context(tc.tile_pool(name="sb", bufs=1))
        ps = ctx.enter_context(tc.psum_pool(name="ps", bufs=1))

        def sbuf(name, shape, dtype, buffer=None):
            return sb.tile(shape, dtype, name=name, tag=buffer or name, align_bytes=64)

        def bank(name, shape, number):
            return ps.tile(shape, F32, name=name, tag="bank%d" % number)

        def load_scales(window, scales):
            for quad in range(4):
                nc.sync.dma_start(
                    out=window[32 * quad : 32 * quad + 4, :].bitcast(I32),
                    in_=scales[0, 4 * quad : 4 * quad + 4, :].bitcast(I32),
                )

        def interleave(engine_copy, dst, src):
            engine_copy(
                out=dst.rearrange("p (c i) t -> p c t i", i=4),
                in_=src.rearrange("p t (c i) -> p c t i", i=4),
            )

        def quantise(codes, scales, values):
            nc.vector.quantize_mx(out=codes.bitcast(FP8X4), scales=scales,
                                  in_=values.rearrange("p c t -> p (c t)"))

        tok_list = lists.tile([P, I // 16], U16, name="tok_list")
        gate_list = lists.tile([P, I // 16], U16, name="gate_list")

        warm_in = sbuf("warm_in", [P, 1], F32, "tw_pool")
        warm_out = sbuf("warm_out", [P, 1], F32, "w_raw0")
        warm_sum = sbuf("warm_sum", [P, 1], F32, "w_raw1")
        warm_bias = sbuf("warm_bias", [P, 1], F32, "ts_pool")
        nc.vector.memset(warm_in[:], 0.0)
        nc.vector.memset(warm_bias[:], 0.0)
        nc.scalar.activation(warm_out[:], warm_in[:], ACT.Exp, bias=warm_bias[:], accum_out=warm_sum[:])

        ks_pool = sbuf("ks_pool", [P, T], U8)
        ts_pool = sbuf("ts_pool", [P, T], U8)
        nc.vector.memset(ks_pool[:].bitcast(I32), 0)
        nc.vector.memset(ts_pool[:].bitcast(I32), 0)
        vs_col = sbuf("vs_col", [P, PACK], F32)
        os_col = sbuf("os_col", [P, PACK], F32)
        nc.gpsimd.dma_start(out=vs_col[:], in_=vs_in.rearrange("o (p t) -> (o p) t", t=PACK))
        nc.gpsimd.dma_start(out=os_col[:], in_=os_in.rearrange("o (p t) -> (o p) t", t=PACK))
        ident = sbuf("ident", [P, P], F32)
        make_identity(nc, ident[:])

        kw_pool = sbuf("kw_pool", [P, T], U16)
        tw_pool = sbuf("tw_pool", [P, T], U16)
        q_raw = sbuf("q_raw", [P, PACK, Q], F32)
        w_raw = [sbuf("w_raw%d" % h, [P, PACK, HALF], F32) for h in range(2)]
        w1_rows = w1.rearrange("(p t) r -> p t r", t=PACK)
        nc.sync.dma_start(tok_list[:], offs)
        nc.sync.dma_start(out=kw_pool[:].bitcast(I32), in_=keys_words[0].bitcast(I32))
        nc.sync.dma_start(gate_list[:], offs2)
        nc.sync.dma_start(out=q_raw[:], in_=query.rearrange("(p t) q -> p t q", t=PACK))
        load_scales(ks_pool, keys_scales)
        nc.sync.dma_start(out=tw_pool[:].bitcast(I32), in_=tab_words[0].bitcast(I32))
        for h in range(2):
            nc.sync.dma_start(out=w_raw[h][:], in_=w1_rows[:, :, h * HALF : (h + 1) * HALF])
        load_scales(ts_pool, tab_scales)

        g_pool = []

        def load_gates(freed_buffer):
            j = len(g_pool)
            g_pool.append(sbuf("g_pool", [P, U], F32, freed_buffer))
            nc.sync.dma_start(out=g_pool[j][:], in_=gtab[j * P : (j + 1) * P, :])

        kw = sbuf("kw", [P, I], U16)
        ks = sbuf("ks", [P, I], U8)
        nc.vector.tensor_copy(kw[:], kw_pool[:].indirect(tok_list[:]))
        load_gates("kw_pool")
        q_bf = sbuf("q_bf", [P, Q, PACK], BF16)
        interleave(nc.scalar.copy, q_bf[:], q_raw[:])
        load_gates("q_raw")
        nc.vector.tensor_copy(ks[:], ks_pool[:].indirect(tok_list[:]))
        load_gates("ks_pool")

        q_codes = sbuf("q_codes", [P, Q], U32)
        q_scales = sbuf("q_scales", [P, Q], U8)
        quantise(q_codes[:], q_scales[:], q_bf[:])
        scores = bank("scores", [P, I], 0)
        nc.tensor.matmul_mx(out=scores[:], lhsT=q_codes[:].bitcast(FP8X4), lhsT_scale=q_scales[:],
                            rhs=kw[:].bitcast(FP4X4), rhs_scale=ks[:], start=True, stop=True)

        tw = sbuf("tw", [P, I], U16)
        nc.vector.tensor_copy(tw[:], tw_pool[:].indirect(tok_list[:]))
        load_gates("tw_pool")

        w_bf = [sbuf("w_bf%d" % h, [P, HALF, PACK], BF16) for h in range(2)]
        interleave(nc.scalar.copy, w_bf[0][:], w_raw[0][:])

        neg_max = sbuf("neg_max", [P, 1], F32)
        nc.vector.tensor_reduce(out=neg_max[:], in_=scores[:], axis=AXIS_X, op=MAX, negate=True)
        probs = sbuf("probs", [P, 2, P, 2], F32, "w_raw0")
        row_sum = sbuf("row_sum", [P, 1], F32)
        nc.scalar.activation(probs[:], scores[:].rearrange("q (s u e) -> q u s e", u=2, e=2), ACT.Exp,
                             bias=neg_max[:], accum_out=row_sum[:])

        gates = sbuf("gates", [P, NBLK, I], F32, "neg_max")
        for j in range(NBLK):
            nc.scalar.activation(gates[:, j, :], g_pool[j][:].indirect(gate_list[:]), ACT.Sigmoid)

        tw_dealt = sbuf("tw_dealt", [P, PACK, P], U16)
        nc.vector.tensor_copy(out=tw_dealt[:], in_=tw[:].rearrange("p (s t) -> p t s", t=PACK))
        ts = sbuf("ts", [P, I], U8, "tw")
        nc.vector.tensor_copy(ts[:], ts_pool[:].indirect(tok_list[:]))
        w_codes = [sbuf("w_codes%d" % h, [P, HALF], U32) for h in range(2)]
        w_scales = [sbuf("w_scales%d" % h, [P, HALF], U8) for h in range(2)]
        quantise(w_codes[0][:], w_scales[0][:], w_bf[0][:])
        ts_dealt = sbuf("ts_dealt", [P, PACK, P], U8)
        nc.vector.tensor_copy(out=ts_dealt[:], in_=ts[:].rearrange("p (s t) -> p t s", t=PACK))
        interleave(nc.vector.tensor_copy, w_bf[1][:], w_raw[1][:])
        inv_sum = sbuf("inv_sum", [P, 1], F32)
        nc.vector.reciprocal(out=inv_sum[:], in_=row_sum[:])
        quantise(w_codes[1][:], w_scales[1][:], w_bf[1][:])

        zv = []
        for j in range(NBLK):
            h, cols = j // 2, slice(j % 2 * P, (j % 2 + 1) * P)
            zh = bank("zh", [P, PACK, P], 2 + j)
            for t in range(PACK):
                nc.tensor.matmul_mx(out=zh[:, t, :], lhsT=tw_dealt[:, t, :].bitcast(FP4X4),
                                    lhsT_scale=ts_dealt[:, t, :], rhs=w_codes[h][:, cols].bitcast(FP8X4),
                                    rhs_scale=w_scales[h][:, cols], start=True, stop=True)
            zv.append(sbuf("zv%d" % j, [P, P, PACK], F32))
            nc.vector.tensor_tensor(out=zv[j][:], in0=zh[:].rearrange("p t r -> p r t"),
                                    in1=vs_col[:].unsqueeze(1).to_broadcast([P, P, PACK]), op=MULT)

        os_rows = bank("os_rows", [P, PACK, P], 2)
        for t in range(PACK):
            nc.tensor.transpose(os_rows[:, t, :], os_col[:, t : t + 1].to_broadcast([P, P]), ident[:])
        wo_bf = sbuf("wo_bf", [P, 2, P, 2], BF16)
        wo_words = wo_bf[:].rearrange("q u s e -> q u (s e)").bitcast(F32)
        wo_turned = bank("wo_turned", [P, 2, Q], 1)
        for u in range(2):
            nc.vector.scalar_tensor_tensor(
                out=wo_bf[:, u], in0=probs[:, u], scalar=inv_sum[:],
                in1=os_rows[:, 2 * u : 2 * u + 2, :].rearrange("q e s -> q s e"), op0=MULT, op1=MULT)
            nc.tensor.transpose(wo_turned[:, u, :], wo_words[:, u, :], ident[:])

        h_bf = sbuf("h_bf", [P, R, PACK], BF16)
        h_codes = sbuf("h_codes", [P, R], U32)
        h_scales = sbuf("h_scales", [P, R], U8)

        def gate_block(j):
            turned = bank("turned", [P, PACK, P], 2 + (j + 1) % NBLK)
            for t in range(PACK):
                nc.tensor.transpose(turned[:, t, :], gates[:, j, t::PACK], ident[:])
            nc.vector.tensor_tensor(out=h_bf[:, j * P : (j + 1) * P, :], in0=turned[:].rearrange("p t r -> p r t"),
                                    in1=zv[j][:], op=MULT)

        def quantise_h(cols):
            quantise(h_codes[:, cols], h_scales[:, cols], h_bf[:, cols, :])

        wt_bf = sbuf("wt_bf", [P, Q, PACK], BF16, "tw_pool")
        wt_codes = sbuf("wt_codes", [P, Q], U32)
        wt_scales = sbuf("wt_scales", [P, Q], U8)
        result = [sbuf("result%d" % h, [P, HALF], F32) for h in range(2)]

        def read_out(cols, bank_number, copy_out):
            width = cols.stop - cols.start
            acc = bank("acc", [P, width], bank_number)
            nc.tensor.matmul_mx(out=acc[:], lhsT=wt_codes[:].bitcast(FP8X4), lhsT_scale=wt_scales[:],
                                rhs=h_codes[:, cols].bitcast(FP8X4), rhs_scale=h_scales[:, cols],
                                start=True, stop=True)
            h, first = divmod(cols.start, HALF)
            copy_out(out=result[h][:, first : first + width], in_=acc[:])

        gate_block(0)
        gate_block(1)
        nc.scalar.copy(out=wt_bf[:].bitcast(F32), in_=wo_turned[:].rearrange("s u q -> s q u"))
        gate_block(2)
        quantise_h(slice(0, HALF))
        quantise(wt_codes[:], wt_scales[:], wt_bf[:])
        read_out(slice(0, HALF), 6, nc.scalar.copy)
        nc.sync.dma_start(out=out[:, :HALF], in_=result[0][:])
        quantise_h(slice(2 * P, 3 * P))
        read_out(slice(2 * P, 3 * P), 7, nc.scalar.copy)
        gate_block(3)
        quantise_h(slice(3 * P, R))
        read_out(slice(3 * P, R), 1, nc.vector.tensor_copy)
        nc.sync.dma_start(out=out[:, HALF:], in_=result[1][:])
